import numpy as np, ml_dtypes
CORES = [16,32,48,64,80]
N = 5
import mx_ref
NC = 256
BF = ml_dtypes.bfloat16
def setup_inputs(rng):
    def f(*shape):
        return mx_ref.flush((rng.standard_normal(shape, dtype=np.float32) * np.exp2(rng.integers(-2, 3, shape[:-1] + (1,)))).astype(BF))
    return {"x": f(N, 128, 512), "rt": f(N, 128, 512), "w": f(N, 128, 4 * NC)}
def setup_inputs_blocks(rng):
    d = setup_inputs(rng)
    for k in ("x", "rt", "w"): d[k] = mx_ref.spread(d[k], rng, 4)
    return d
def setup_inputs_wide(rng):
    d = setup_inputs(rng)
    for k in ("x", "rt", "w"): d[k] = mx_ref.flush((d[k].astype(np.float32) * np.exp2(rng.integers(-6, 7, (N, 1, 1))).astype(np.float32)).astype(BF))
    return d
def setup_inputs_near(rng):
    d = setup_inputs(rng); v = d["rt"].astype(np.float32).reshape(N, 128, -1, 4)
    d["rt"] = mx_ref.flush((v[:, :, :1] + v / 64).reshape(d["rt"].shape).astype(BF))
    return d
def setup_inputs_twins(rng):
    d = setup_inputs(rng); v = d["rt"].reshape(N, 128, -1, 4).copy()
    v[:, :, 1] = v[:, :, 0]
    d["rt"] = v.reshape(d["rt"].shape)
    return d
def reference(x, rt, w):
    W = [mx_ref.quantize(w[e]) for e in range(N)]
    y = np.zeros((N, 128, NC), np.float32)
    for j in range(N):
        X = mx_ref.quantize(x[j])
        lg = mx_ref.matmul(X, mx_ref.quantize(rt[j]))[:, :N]
        m = lg.max(axis=1, keepdims=True)
        for e in range(N):
            y[j] = y[j] + (lg[:, e:e + 1] == m) * (mx_ref.matmul(X, W[e]) * m)
    return {"y": y}

@@ -1,0 +1,165 @@
+from concourse.bass import DstId, RemoteDMATransfer
+from concourse.mybir import dt, AluOpType, AxisListType, ActivationFunctionType
+
+N = 5
+NC = 256
+NT = 128
+
+DIRECT = (1, 2, 3)
+RELAY = ((4,),)
+ORDER = (1, 2, 3, 4)
+
+SCRATCH = {
+    "wb": ("sbuf", [128, 4 * NC], "bfloat16"),
+    "xb": ("sbuf", [128, 4 * NT], "bfloat16"),
+    "rb": ("sbuf", [128, 4 * NT], "bfloat16"),
+    "wq": ("sbuf", [128, NC], "float8_e4m3fn_x4"),
+    "ws": ("sbuf", [128, NC], "uint8"),
+    "xq": ("sbuf", [128, NT], "float8_e4m3fn_x4"),
+    "xs": ("sbuf", [128, NT], "uint8"),
+    "rq": ("sbuf", [128, NT], "float8_e4m3fn_x4"),
+    "rs": ("sbuf", [128, NT], "uint8"),
+    "gq": ("sbuf", [128, (N - 1) * NC], "float8_e4m3fn_x4"),
+    "gs": ("sbuf", [128, (N - 1) * NC], "uint8"),
+    "pl": ("psum", [128, 512], "float32"),
+    "pw": ("psum", [128, 512 * N], "float32"),
+    "mx": ("sbuf", [128, 4], "float32"),
+    "sel": ("sbuf", [128, 8], "float32"),
+    "tmp": ("sbuf", [128, (N - 1) * NC], "float32"),
+    "acc": ("sbuf", [128, NC], "float32"),
+}
+SEMAPHORES = (["ldw", "ldx", "ldr", "qw", "qx", "ml", "mo", "vm", "vs", "va0", "st", "sent", "hs", "hc", "sc"]
+              + ["arr%d" % d for d in range(1, N)] + ["mm%d" % d for d in range(1, N)]
+              + ["sm%d" % d for d in range(1, N)] + ["va%d" % d for d in range(1, N)])
+
+
+def _count(mask):
+    return bin(mask).count("1")
+
+
+def _slot(d):
+    return slice((d - 1) * NC, d * NC)
+
+
+def _relays(rank, cores, topo):
+    own = cores[rank]
+    pool = [c for c in range(topo.CHIPS * topo.CORES_PER_CHIP)
+            if topo.chip(c) == topo.chip(own) and topo.die(c) != topo.die(own) and c not in cores
+            and all(topo.may_write(c, o) for o in cores)]
+    return pool[:len(RELAY)]
+
+
+def _relay_program(g, core, rank, mine, T, topo, hop):
+    S, cores = T.sem, list(T.cores)
+    total = 0
+    for sem, src, land in ((S.hs, T.ws[:], lambda d: T.gs[:, _slot(d)]),
+                           (S.hc, T.wq[:].bitcast(dt.uint8), lambda d: T.gq[:, _slot(d)].bitcast(dt.uint8))):
+        g.wait_ge(sem, hop)
+        for d in mine:
+            dst = cores[(rank + d) % N]
+            rid, pid, _ = topo.addr(dst)
+            mask = topo.mask(core, dst)
+            g.remote_dma(out_ap=land(d), in_ap=src, remote_sem=S["arr%d" % d], local_sem=S.sent,
+                         pid=pid, routing_id=rid, dma_engine_mask=mask)
+            total += _count(mask)
+    g.wait_ge(S.sent, total)
+
+
+def rank_program(g, core, T, topo):
+    S, cores = T.sem, list(T.cores)
+
+    def did(c):
+        rid, pid, _ = topo.addr(c)
+        return DstId(rid=rid, pnc=pid)
+
+    def engines(rank):
+        own = cores[rank]
+        far = topo.mask(own, cores[(rank + 1) % N])
+        near = 0
+        for h in _relays(rank, cores, topo):
+            near = topo.mask(own, h) & ~far
+        return far, near
+
+    rank = T.rank_of(core)
+    if rank is None:
+        for r in range(N):
+            hs = _relays(r, cores, topo)
+            if core in hs:
+                _relay_program(g, core, r, RELAY[hs.index(core)], T, topo, _count(engines(r)[1]))
+        return
+
+    far, near = engines(rank)
+    helpers = _relays(rank, cores, topo)
+    relayed = [d for mine in RELAY for d in mine]
+
+    g.sync.dma_start(T.wb[:], T.w[:]).then_inc(S.ldw, 16)
+    g.sync.dma_start(T.xb[:], T.x[:]).then_inc(S.ldx, 16)
+    g.sync.dma_start(T.rb[:], T.rt[:]).then_inc(S.ldr, 16)
+
+    g.vector.wait_ge(S.ldw, 16)
+    g.vector.quantize_mx(T.wq[:], T.ws[:], T.wb[:]).then_inc(S.qw, 1)
+    g.vector.wait_ge(S.ldx, 16)
+    g.vector.quantize_mx(T.xq[:], T.xs[:], T.xb[:]).then_inc(S.qx, 1)
+    g.vector.wait_ge(S.ldr, 16)
+    g.vector.quantize_mx(T.rq[:], T.rs[:], T.rb[:]).then_inc(S.qx, 1)
+
+    g.wait_ge(S.qw, 1)
+    sent = 0
+    tr = []
+    if helpers:
+        tr.append(RemoteDMATransfer(dst_ids=[did(h) for h in helpers], dma_engine_mask=near, remote_sem=S.hs,
+                                    srcs=[T.ws[:]], dsts=[T.ws[:] for h in helpers]))
+        sent += _count(near)
+    tr.append(RemoteDMATransfer(dst_ids=[did(cores[(rank + d) % N]) for d in DIRECT], dma_engine_mask=far,
+                                remote_sem=S.sc, srcs=[T.ws[:]], dsts=[T.gs[:, _slot(d)] for d in DIRECT]))
+    sent += _count(far)
+    g.remote_dma_fused(tr, local_sem=S.sent)
+    for k, d in enumerate(DIRECT):
+        tr = []
+        if helpers and k == 0:
+            tr.append(RemoteDMATransfer(dst_ids=[did(h) for h in helpers], dma_engine_mask=near, remote_sem=S.hc,
+                                        srcs=[T.wq[:].bitcast(dt.uint8)],
+                                        dsts=[T.wq[:].bitcast(dt.uint8) for h in helpers]))
+            sent += _count(near)
+        tr.append(RemoteDMATransfer(dst_ids=[did(cores[(rank + d) % N])], dma_engine_mask=far,
+                                    remote_sem=S["arr%d" % d], srcs=[T.wq[:].bitcast(dt.uint8)],
+                                    dsts=[T.gq[:, _slot(d)].bitcast(dt.uint8)]))
+        sent += _count(far)
+        g.remote_dma_fused(tr, local_sem=S.sent)
+
+    g.tensor.wait_ge(S.qx, 2)
+    g.tensor.matmul_mx(T.pl[:, 0:NT], T.xq[:], T.xs[:], T.rq[:], T.rs[:], True, True).then_inc(S.ml, 1)
+    g.tensor.wait_ge(S.qw, 1)
+    g.tensor.matmul_mx(T.pw[:, 0:NC], T.xq[:], T.xs[:], T.wq[:], T.ws[:], True, True).then_inc(S.mo, 1)
+    g.tensor.wait_ge(S.sc, _count(far) * len(DIRECT))
+    for d in ORDER:
+        g.tensor.wait_ge(S["arr%d" % d], _count(far) * (2 if d in relayed else 1))
+        g.tensor.matmul_mx(T.pw[:, 512 * d:512 * d + NC], T.xq[:], T.xs[:], T.gq[:, _slot(d)], T.gs[:, _slot(d)],
+                           True, True).then_inc(S["mm%d" % d], 1)
+
+    g.vector.wait_ge(S.ml, 1)
+    g.vector.tensor_reduce(T.mx[:, 0:1], T.pl[:, 0:N], AxisListType.X, AluOpType.max).then_inc(S.vm, 1)
+    g.vector.wait_ge(S.vm, 1)
+    g.vector.tensor_scalar(T.sel[:, 0:N], T.pl[:, 0:N], T.mx[:, 0:1], T.mx[:, 0:1],
+                           AluOpType.is_equal, AluOpType.mult).then_inc(S.vs, 1)
+    g.vector.wait_ge(S.vs, 1)
+    g.vector.wait_ge(S.mo, 1)
+    g.vector.tensor_scalar(T.acc[:], T.pw[:, 0:NC], T.sel[:, rank:rank + 1], 0.0,
+                           AluOpType.mult, AluOpType.add).then_inc(S.va0, 1)
+
+    g.scalar.wait_ge(S.vs, 1)
+    last = S.va0
+    for d in ORDER:
+        e = (rank - d) % N
+        g.scalar.wait_ge(S["mm%d" % d], 1)
+        g.scalar.activation(T.tmp[:, _slot(d)], T.pw[:, 512 * d:512 * d + NC], ActivationFunctionType.Copy,
+                            scale=T.sel[:, e:e + 1]).then_inc(S["sm%d" % d], 1)
+        g.vector.wait_ge(last, 1)
+        g.vector.wait_ge(S["sm%d" % d], 1)
+        last = S["va%d" % d]
+        g.vector.tensor_tensor(T.acc[:], T.acc[:], T.tmp[:, _slot(d)], AluOpType.add).then_inc(last, 1)
+
+    g.sync.wait_ge(last, 1)
+    g.sync.dma_start(T.y[:], T.acc[:]).then_inc(S.st, 16)
+    g.sync.wait_ge(S.st, 16)
+    g.wait_ge(S.sent, sent)

@@ -4,10 +4,13 @@ from concourse.mybir import dt, AluOpType, AxisListType, ActivationFunctionType
 N = 5
 NC = 256
 NT = 128
+HALF = NC // 2
 
-DIRECT = (1, 2, 3)
-RELAY = ((4,),)
-ORDER = (1, 2, 3, 4)
+R_PLANES = (1, 2)
+R_CODES = ((1, 0, NC), (2, 0, NC), (3, 0, HALF))
+H_PLANES = (4, 3)
+H_CODES = ((4, 0, NC), (3, HALF, NC))
+TAKE = ((1, 0, NC), (2, 0, NC), (3, 0, HALF), (4, 0, NC), (3, HALF, NC))
 
 SCRATCH = {
     "wb": ("sbuf", [128, 4 * NC], "bfloat16"),
@@ -22,75 +25,74 @@ SCRATCH = {
     "gq": ("sbuf", [128, (N - 1) * NC], "float8_e4m3fn_x4"),
     "gs": ("sbuf", [128, (N - 1) * NC], "uint8"),
     "pl": ("psum", [128, 512], "float32"),
-    "pw": ("psum", [128, 512 * N], "float32"),
+    "pw": ("psum", [128, 512 * (1 + len(TAKE))], "float32"),
     "mx": ("sbuf", [128, 4], "float32"),
     "sel": ("sbuf", [128, 8], "float32"),
     "tmp": ("sbuf", [128, (N - 1) * NC], "float32"),
     "acc": ("sbuf", [128, NC], "float32"),
 }
-SEMAPHORES = (["ldw", "ldx", "ldr", "qw", "qx", "ml", "mo", "vm", "vs", "va0", "st", "sent", "hs", "hc", "sc"]
-              + ["arr%d" % d for d in range(1, N)] + ["mm%d" % d for d in range(1, N)]
-              + ["sm%d" % d for d in range(1, N)] + ["va%d" % d for d in range(1, N)])
+SEMAPHORES = (["ldw", "ldx", "ldr", "qw", "qx", "ml", "mo", "vm", "vs", "va", "st", "sent", "hs", "hc", "sc", "sh"]
+              + ["%s%d" % (n, k) for n in ("ar", "mm", "sm", "va") for k in range(len(TAKE))])
 
 
 def _count(mask):
     return bin(mask).count("1")
 
 
-def _slot(d):
-    return slice((d - 1) * NC, d * NC)
+def _cols(piece):
+    d, a, b = piece
+    return slice((d - 1) * NC + a, (d - 1) * NC + b)
 
 
-def _relays(rank, cores, topo):
+def _relay(rank, cores, topo):
     own = cores[rank]
-    pool = [c for c in range(topo.CHIPS * topo.CORES_PER_CHIP)
+    return [c for c in range(topo.CHIPS * topo.CORES_PER_CHIP)
             if topo.chip(c) == topo.chip(own) and topo.die(c) != topo.die(own) and c not in cores
-            and all(topo.may_write(c, o) for o in cores)]
-    return pool[:len(RELAY)]
+            and all(topo.may_write(c, o) for o in cores)][0]
 
 
-def _relay_program(g, core, rank, mine, T, topo, hop):
+def _send(g, T, topo, core, rank, planes, codes, plane_sem, ride_planes, ride_codes):
     S, cores = T.sem, list(T.cores)
-    total = 0
-    for sem, src, land in ((S.hs, T.ws[:], lambda d: T.gs[:, _slot(d)]),
-                           (S.hc, T.wq[:].bitcast(dt.uint8), lambda d: T.gq[:, _slot(d)].bitcast(dt.uint8))):
-        g.wait_ge(sem, hop)
-        for d in mine:
-            dst = cores[(rank + d) % N]
-            rid, pid, _ = topo.addr(dst)
-            mask = topo.mask(core, dst)
-            g.remote_dma(out_ap=land(d), in_ap=src, remote_sem=S["arr%d" % d], local_sem=S.sent,
-                         pid=pid, routing_id=rid, dma_engine_mask=mask)
-            total += _count(mask)
-    g.wait_ge(S.sent, total)
+
+    def did(d):
+        rid, pid, _ = topo.addr(cores[(rank + d) % N])
+        return DstId(rid=rid, pnc=pid)
+
+    far = topo.mask(core, cores[(rank + 1) % N])
+    tr = list(ride_planes)
+    tr.append(RemoteDMATransfer(dst_ids=[did(d) for d in planes], dma_engine_mask=far, remote_sem=plane_sem,
+                                srcs=[T.ws[:]], dsts=[T.gs[:, _cols((d, 0, NC))] for d in planes]))
+    g.remote_dma_fused(tr, local_sem=S.sent)
+    yield _count(far)
+    for k, p in enumerate(codes):
+        tr = list(ride_codes) if k == 0 else []
+        tr.append(RemoteDMATransfer(dst_ids=[did(p[0])], dma_engine_mask=far, remote_sem=S["ar%d" % TAKE.index(p)],
+                                    srcs=[T.wq[:, p[1]:p[2]].bitcast(dt.uint8)],
+                                    dsts=[T.gq[:, _cols(p)].bitcast(dt.uint8)]))
+        g.remote_dma_fused(tr, local_sem=S.sent)
+        yield _count(far)
 
 
 def rank_program(g, core, T, topo):
     S, cores = T.sem, list(T.cores)
-
-    def did(c):
-        rid, pid, _ = topo.addr(c)
-        return DstId(rid=rid, pnc=pid)
-
-    def engines(rank):
-        own = cores[rank]
-        far = topo.mask(own, cores[(rank + 1) % N])
-        near = 0
-        for h in _relays(rank, cores, topo):
-            near = topo.mask(own, h) & ~far
-        return far, near
-
     rank = T.rank_of(core)
+
     if rank is None:
         for r in range(N):
-            hs = _relays(r, cores, topo)
-            if core in hs:
-                _relay_program(g, core, r, RELAY[hs.index(core)], T, topo, _count(engines(r)[1]))
+            if core == _relay(r, cores, topo):
+                near = topo.mask(cores[r], core) & ~topo.mask(cores[r], cores[(r + 1) % N])
+                steps = _send(g, T, topo, core, r, H_PLANES, H_CODES, S.sh, [], [])
+                g.wait_ge(S.hs, _count(near))
+                sent = next(steps)
+                g.wait_ge(S.hc, _count(near))
+                sent += sum(steps)
+                g.wait_ge(S.sent, sent)
         return
 
-    far, near = engines(rank)
-    helpers = _relays(rank, cores, topo)
-    relayed = [d for mine in RELAY for d in mine]
+    helper = _relay(rank, cores, topo)
+    far = topo.mask(core, cores[(rank + 1) % N])
+    near = topo.mask(core, helper) & ~far
+    hrid, hpid, _ = topo.addr(helper)
 
     g.sync.dma_start(T.wb[:], T.w[:]).then_inc(S.ldw, 16)
     g.sync.dma_start(T.xb[:], T.x[:]).then_inc(S.ldx, 16)
@@ -104,38 +106,24 @@ def rank_program(g, core, T, topo):
     g.vector.quantize_mx(T.rq[:], T.rs[:], T.rb[:]).then_inc(S.qx, 1)
 
     g.wait_ge(S.qw, 1)
-    sent = 0
-    tr = []
-    if helpers:
-        tr.append(RemoteDMATransfer(dst_ids=[did(h) for h in helpers], dma_engine_mask=near, remote_sem=S.hs,
-                                    srcs=[T.ws[:]], dsts=[T.ws[:] for h in helpers]))
-        sent += _count(near)
-    tr.append(RemoteDMATransfer(dst_ids=[did(cores[(rank + d) % N]) for d in DIRECT], dma_engine_mask=far,
-                                remote_sem=S.sc, srcs=[T.ws[:]], dsts=[T.gs[:, _slot(d)] for d in DIRECT]))
-    sent += _count(far)
-    g.remote_dma_fused(tr, local_sem=S.sent)
-    for k, d in enumerate(DIRECT):
-        tr = []
-        if helpers and k == 0:
-            tr.append(RemoteDMATransfer(dst_ids=[did(h) for h in helpers], dma_engine_mask=near, remote_sem=S.hc,
-                                        srcs=[T.wq[:].bitcast(dt.uint8)],
-                                        dsts=[T.wq[:].bitcast(dt.uint8) for h in helpers]))
-            sent += _count(near)
-        tr.append(RemoteDMATransfer(dst_ids=[did(cores[(rank + d) % N])], dma_engine_mask=far,
-                                    remote_sem=S["arr%d" % d], srcs=[T.wq[:].bitcast(dt.uint8)],
-                                    dsts=[T.gq[:, _slot(d)].bitcast(dt.uint8)]))
-        sent += _count(far)
-        g.remote_dma_fused(tr, local_sem=S.sent)
+    hop_s = RemoteDMATransfer(dst_ids=[DstId(rid=hrid, pnc=hpid)], dma_engine_mask=near, remote_sem=S.hs,
+                              srcs=[T.ws[:]], dsts=[T.ws[:]])
+    hop_c = RemoteDMATransfer(dst_ids=[DstId(rid=hrid, pnc=hpid)], dma_engine_mask=near, remote_sem=S.hc,
+                              srcs=[T.wq[:].bitcast(dt.uint8)], dsts=[T.wq[:].bitcast(dt.uint8)])
+    sent = 2 * _count(near) + sum(_send(g, T, topo, core, rank, R_PLANES, R_CODES, S.sc, [hop_s], [hop_c]))
 
     g.tensor.wait_ge(S.qx, 2)
     g.tensor.matmul_mx(T.pl[:, 0:NT], T.xq[:], T.xs[:], T.rq[:], T.rs[:], True, True).then_inc(S.ml, 1)
     g.tensor.wait_ge(S.qw, 1)
     g.tensor.matmul_mx(T.pw[:, 0:NC], T.xq[:], T.xs[:], T.wq[:], T.ws[:], True, True).then_inc(S.mo, 1)
-    g.tensor.wait_ge(S.sc, _count(far) * len(DIRECT))
-    for d in ORDER:
-        g.tensor.wait_ge(S["arr%d" % d], _count(far) * (2 if d in relayed else 1))
-        g.tensor.matmul_mx(T.pw[:, 512 * d:512 * d + NC], T.xq[:], T.xs[:], T.gq[:, _slot(d)], T.gs[:, _slot(d)],
-                           True, True).then_inc(S["mm%d" % d], 1)
+    for k, p in enumerate(TAKE):
+        if p[0] in R_PLANES:
+            g.tensor.wait_ge(S.sc, _count(far) * len(R_PLANES))
+        else:
+            g.tensor.wait_ge(S.sh, _count(far) * len(H_PLANES))
+        g.tensor.wait_ge(S["ar%d" % k], _count(far))
+        g.tensor.matmul_mx(T.pw[:, 512 * (k + 1):512 * (k + 1) + p[2] - p[1]], T.xq[:], T.xs[:],
+                           T.gq[:, _cols(p)], T.gs[:, _cols(p)], True, True).then_inc(S["mm%d" % k], 1)
 
     g.vector.wait_ge(S.ml, 1)
     g.vector.tensor_reduce(T.mx[:, 0:1], T.pl[:, 0:N], AxisListType.X, AluOpType.max).then_inc(S.vm, 1)
@@ -145,19 +133,20 @@ def rank_program(g, core, T, topo):
     g.vector.wait_ge(S.vs, 1)
     g.vector.wait_ge(S.mo, 1)
     g.vector.tensor_scalar(T.acc[:], T.pw[:, 0:NC], T.sel[:, rank:rank + 1], 0.0,
-                           AluOpType.mult, AluOpType.add).then_inc(S.va0, 1)
+                           AluOpType.mult, AluOpType.add).then_inc(S.va, 1)
 
     g.scalar.wait_ge(S.vs, 1)
-    last = S.va0
-    for d in ORDER:
-        e = (rank - d) % N
-        g.scalar.wait_ge(S["mm%d" % d], 1)
-        g.scalar.activation(T.tmp[:, _slot(d)], T.pw[:, 512 * d:512 * d + NC], ActivationFunctionType.Copy,
-                            scale=T.sel[:, e:e + 1]).then_inc(S["sm%d" % d], 1)
+    last = S.va
+    for k, p in enumerate(TAKE):
+        e = (rank - p[0]) % N
+        g.scalar.wait_ge(S["mm%d" % k], 1)
+        g.scalar.activation(T.tmp[:, _cols(p)], T.pw[:, 512 * (k + 1):512 * (k + 1) + p[2] - p[1]],
+                            ActivationFunctionType.Copy, scale=T.sel[:, e:e + 1]).then_inc(S["sm%d" % k], 1)
         g.vector.wait_ge(last, 1)
-        g.vector.wait_ge(S["sm%d" % d], 1)
-        last = S["va%d" % d]
-        g.vector.tensor_tensor(T.acc[:], T.acc[:], T.tmp[:, _slot(d)], AluOpType.add).then_inc(last, 1)
+        g.vector.wait_ge(S["sm%d" % k], 1)
+        last = S["va%d" % k]
+        g.vector.tensor_tensor(T.acc[:, p[1]:p[2]], T.acc[:, p[1]:p[2]], T.tmp[:, _cols(p)],
+                               AluOpType.add).then_inc(last, 1)
 
     g.sync.wait_ge(last, 1)
     g.sync.dma_start(T.y[:], T.acc[:]).then_inc(S.st, 16)

from concourse.bass import DstId, RemoteDMATransfer
from concourse.mybir import dt, AluOpType, AxisListType, ActivationFunctionType

N = 5
NC = 256
NT = 128
HALF = NC // 2

R_PLANES = (1, 2)
R_CODES = ((1, 0, NC), (2, 0, NC), (3, 0, HALF))
H_PLANES = (4, 3)
H_CODES = ((4, 0, NC), (3, HALF, NC))
TAKE = ((1, 0, NC), (2, 0, NC), (3, 0, HALF), (4, 0, NC), (3, HALF, NC))

SCRATCH = {
    "wb": ("sbuf", [128, 4 * NC], "bfloat16"),
    "xb": ("sbuf", [128, 4 * NT], "bfloat16"),
    "rb": ("sbuf", [128, 4 * NT], "bfloat16"),
    "wq": ("sbuf", [128, NC], "float8_e4m3fn_x4"),
    "ws": ("sbuf", [128, NC], "uint8"),
    "xq": ("sbuf", [128, NT], "float8_e4m3fn_x4"),
    "xs": ("sbuf", [128, NT], "uint8"),
    "rq": ("sbuf", [128, NT], "float8_e4m3fn_x4"),
    "rs": ("sbuf", [128, NT], "uint8"),
    "gq": ("sbuf", [128, (N - 1) * NC], "float8_e4m3fn_x4"),
    "gs": ("sbuf", [128, (N - 1) * NC], "uint8"),
    "pl": ("psum", [128, 512], "float32"),
    "pw": ("psum", [128, 512 * (1 + len(TAKE))], "float32"),
    "mx": ("sbuf", [128, 4], "float32"),
    "sel": ("sbuf", [128, 8], "float32"),
    "tmp": ("sbuf", [128, (N - 1) * NC], "float32"),
    "acc": ("sbuf", [128, NC], "float32"),
}
SEMAPHORES = (["ldw", "ldx", "ldr", "qw", "qx", "ml", "mo", "vm", "vs", "va", "st", "sent", "hs", "hc", "sc", "sh"]
              + ["%s%d" % (n, k) for n in ("ar", "mm", "sm", "va") for k in range(len(TAKE))])


def _count(mask):
    return bin(mask).count("1")


def _cols(piece):
    d, a, b = piece
    return slice((d - 1) * NC + a, (d - 1) * NC + b)


def _relay(rank, cores, topo):
    own = cores[rank]
    return [c for c in range(topo.CHIPS * topo.CORES_PER_CHIP)
            if topo.chip(c) == topo.chip(own) and topo.die(c) != topo.die(own) and c not in cores
            and all(topo.may_write(c, o) for o in cores)][0]


def _send(g, T, topo, core, rank, planes, codes, plane_sem, ride_planes, ride_codes):
    S, cores = T.sem, list(T.cores)

    def did(d):
        rid, pid, _ = topo.addr(cores[(rank + d) % N])
        return DstId(rid=rid, pnc=pid)

    far = topo.mask(core, cores[(rank + 1) % N])
    tr = list(ride_planes)
    tr.append(RemoteDMATransfer(dst_ids=[did(d) for d in planes], dma_engine_mask=far, remote_sem=plane_sem,
                                srcs=[T.ws[:]], dsts=[T.gs[:, _cols((d, 0, NC))] for d in planes]))
    g.remote_dma_fused(tr, local_sem=S.sent)
    yield _count(far)
    for k, p in enumerate(codes):
        tr = list(ride_codes) if k == 0 else []
        tr.append(RemoteDMATransfer(dst_ids=[did(p[0])], dma_engine_mask=far, remote_sem=S["ar%d" % TAKE.index(p)],
                                    srcs=[T.wq[:, p[1]:p[2]].bitcast(dt.uint8)],
                                    dsts=[T.gq[:, _cols(p)].bitcast(dt.uint8)]))
        g.remote_dma_fused(tr, local_sem=S.sent)
        yield _count(far)


def rank_program(g, core, T, topo):
    S, cores = T.sem, list(T.cores)
    rank = T.rank_of(core)

    if rank is None:
        for r in range(N):
            if core == _relay(r, cores, topo):
                near = topo.mask(cores[r], core) & ~topo.mask(cores[r], cores[(r + 1) % N])
                steps = _send(g, T, topo, core, r, H_PLANES, H_CODES, S.sh, [], [])
                g.wait_ge(S.hs, _count(near))
                sent = next(steps)
                g.wait_ge(S.hc, _count(near))
                sent += sum(steps)
                g.wait_ge(S.sent, sent)
        return

    helper = _relay(rank, cores, topo)
    far = topo.mask(core, cores[(rank + 1) % N])
    near = topo.mask(core, helper) & ~far
    hrid, hpid, _ = topo.addr(helper)

    g.sync.dma_start(T.wb[:], T.w[:]).then_inc(S.ldw, 16)
    g.sync.dma_start(T.xb[:], T.x[:]).then_inc(S.ldx, 16)
    g.sync.dma_start(T.rb[:], T.rt[:]).then_inc(S.ldr, 16)

    g.vector.wait_ge(S.ldw, 16)
    g.vector.quantize_mx(T.wq[:], T.ws[:], T.wb[:]).then_inc(S.qw, 1)
    g.vector.wait_ge(S.ldx, 16)
    g.vector.quantize_mx(T.xq[:], T.xs[:], T.xb[:]).then_inc(S.qx, 1)
    g.vector.wait_ge(S.ldr, 16)
    g.vector.quantize_mx(T.rq[:], T.rs[:], T.rb[:]).then_inc(S.qx, 1)

    g.wait_ge(S.qw, 1)
    hop_s = RemoteDMATransfer(dst_ids=[DstId(rid=hrid, pnc=hpid)], dma_engine_mask=near, remote_sem=S.hs,
                              srcs=[T.ws[:]], dsts=[T.ws[:]])
    hop_c = RemoteDMATransfer(dst_ids=[DstId(rid=hrid, pnc=hpid)], dma_engine_mask=near, remote_sem=S.hc,
                              srcs=[T.wq[:].bitcast(dt.uint8)], dsts=[T.wq[:].bitcast(dt.uint8)])
    sent = 2 * _count(near) + sum(_send(g, T, topo, core, rank, R_PLANES, R_CODES, S.sc, [hop_s], [hop_c]))

    g.tensor.wait_ge(S.qx, 2)
    g.tensor.matmul_mx(T.pl[:, 0:NT], T.xq[:], T.xs[:], T.rq[:], T.rs[:], True, True).then_inc(S.ml, 1)
    g.tensor.wait_ge(S.qw, 1)
    g.tensor.matmul_mx(T.pw[:, 0:NC], T.xq[:], T.xs[:], T.wq[:], T.ws[:], True, True).then_inc(S.mo, 1)
    for k, p in enumerate(TAKE):
        if p[0] in R_PLANES:
            g.tensor.wait_ge(S.sc, _count(far) * len(R_PLANES))
        else:
            g.tensor.wait_ge(S.sh, _count(far) * len(H_PLANES))
        g.tensor.wait_ge(S["ar%d" % k], _count(far))
        g.tensor.matmul_mx(T.pw[:, 512 * (k + 1):512 * (k + 1) + p[2] - p[1]], T.xq[:], T.xs[:],
                           T.gq[:, _cols(p)], T.gs[:, _cols(p)], True, True).then_inc(S["mm%d" % k], 1)

    g.vector.wait_ge(S.ml, 1)
    g.vector.tensor_reduce(T.mx[:, 0:1], T.pl[:, 0:N], AxisListType.X, AluOpType.max).then_inc(S.vm, 1)
    g.vector.wait_ge(S.vm, 1)
    g.vector.tensor_scalar(T.sel[:, 0:N], T.pl[:, 0:N], T.mx[:, 0:1], T.mx[:, 0:1],
                           AluOpType.is_equal, AluOpType.mult).then_inc(S.vs, 1)
    g.vector.wait_ge(S.vs, 1)
    g.vector.wait_ge(S.mo, 1)
    g.vector.tensor_scalar(T.acc[:], T.pw[:, 0:NC], T.sel[:, rank:rank + 1], 0.0,
                           AluOpType.mult, AluOpType.add).then_inc(S.va, 1)

    g.scalar.wait_ge(S.vs, 1)
    last = S.va
    for k, p in enumerate(TAKE):
        e = (rank - p[0]) % N
        g.scalar.wait_ge(S["mm%d" % k], 1)
        g.scalar.activation(T.tmp[:, _cols(p)], T.pw[:, 512 * (k + 1):512 * (k + 1) + p[2] - p[1]],
                            ActivationFunctionType.Copy, scale=T.sel[:, e:e + 1]).then_inc(S["sm%d" % k], 1)
        g.vector.wait_ge(last, 1)
        g.vector.wait_ge(S["sm%d" % k], 1)
        last = S["va%d" % k]
        g.vector.tensor_tensor(T.acc[:, p[1]:p[2]], T.acc[:, p[1]:p[2]], T.tmp[:, _cols(p)],
                               AluOpType.add).then_inc(last, 1)

    g.sync.wait_ge(last, 1)
    g.sync.dma_start(T.y[:], T.acc[:]).then_inc(S.st, 16)
    g.sync.wait_ge(S.st, 16)
    g.wait_ge(S.sent, sent)
